import numpy as np
import ml_dtypes


def mxq(x, axis, fmt="e4m3"):
    dtype, down = {"e4m3": (ml_dtypes.float8_e4m3fn, 7), "e5m2": (ml_dtypes.float8_e5m2, 14)}[fmt]
    v = np.moveaxis(np.asarray(x, np.float32).astype(ml_dtypes.bfloat16).astype(np.float64), axis, -1)
    blocks = v.reshape(v.shape[:-1] + (-1, 32))
    amax = np.abs(blocks).max(-1, keepdims=True)
    byte = np.maximum(np.where(amax > 0, np.frexp(amax)[1] - 1 + 127, 0) - down, 1)
    scale = np.exp2(byte - 127.0)
    codes = (blocks / scale).astype(np.float32).astype(dtype).astype(np.float64)
    return np.moveaxis((codes * scale).reshape(v.shape), -1, axis)


WIDE = False


def mx_kscale(k):
    if not WIDE:
        return np.ones(k)
    levels = np.array([30, -30])
    if k % 512:
        return np.exp2(np.random.permutation(np.resize(levels, k // 32))).repeat(32)
    a = np.empty((k // 512, 16))
    for p in range(k // 512):
        a[p, :8] = np.random.permutation(np.resize(levels, 8))
        for g in range(8):
            far = levels[np.abs(levels - a[p, g]) >= 10]
            a[p, g + 8] = far[np.random.randint(len(far))]
    return np.exp2(a.ravel()).repeat(32)


def f64(x):
    return np.asarray(x).astype(np.float64)


def striped(idx):
    return np.tile(np.asarray(idx).reshape(-1, 16).T, (8, 1)).astype(np.uint16)


def unstriped(offs):
    return offs[:16].T.reshape(-1).astype(np.int64)


E2M1 = np.array([0.0, 0.5, 1.0, 1.5, 2.0, 3.0, 4.0, 6.0, -0.0, -0.5, -1.0, -1.5, -2.0, -3.0, -4.0, -6.0])


def pack_weight(w, fmt):
    k, n = w.shape
    w = f64(np.asarray(w, np.float32).astype(ml_dtypes.bfloat16)).reshape(k // 32, 32, n)
    amax = np.abs(w).max(1)
    if fmt == "e4m3":
        byte = np.frexp(amax)[1] - 1 + 127 - 7
    else:
        mant, ex = np.frexp(amax / 6.0)
        byte = np.where(mant > 0.5, ex, ex - 1) + 127
    byte = np.clip(np.where(amax > 0, byte, 1), 1, 254)
    scaled = (w * np.exp2(127.0 - byte)[:, None, :]).reshape(k, n).astype(np.float32)
    by_word = np.ascontiguousarray(scaled.reshape(k // 512, 128, 4, n).transpose(0, 1, 3, 2))
    if fmt == "e4m3":
        words = by_word.astype(ml_dtypes.float8_e4m3fn).view(np.uint8)
    else:
        c = by_word.astype(ml_dtypes.float4_e2m1fn).view(np.uint8) & 0xF
        words = (c[..., 0::2] | (c[..., 1::2] << 4)).reshape(k // 512, 128, 2 * n)
    return np.ascontiguousarray(words), np.ascontiguousarray(byte.astype(np.uint8).reshape(k // 512, 16, n))


def unpack_weight(words, scales, fmt):
    g, _, n = scales.shape
    words = np.ascontiguousarray(words).reshape(g, 128, n, -1)
    if fmt == "e4m3":
        vals = words.view(ml_dtypes.float8_e4m3fn).astype(np.float64)
    else:
        nib = np.empty((g, 128, n, 4), np.uint8)
        nib[..., 0::2] = words & 0xF
        nib[..., 1::2] = words >> 4
        vals = E2M1[nib]
    vals = vals * np.repeat(np.exp2(scales.astype(np.float64) - 127.0), 8, axis=1)[..., None]
    return vals.transpose(0, 1, 3, 2).reshape(g * 512, n)


def bf(x):
    return np.asarray(x, np.float32).astype(ml_dtypes.bfloat16)


def planes(Y):
    r, m = Y.shape
    b = f64(bf(Y)).reshape(r // 32, 32, m)
    amax = np.abs(b).max(1)
    byte = np.clip(np.where(amax > 0, np.frexp(amax)[1] - 1 + 127 - 7, 1), 1, 254)
    codes = (b * np.exp2(127.0 - byte)[:, None, :]).reshape(r, m).astype(np.float32).astype(ml_dtypes.float8_e4m3fn).view(np.uint8)
    words = codes.reshape(r // 512, 128, 4, m).transpose(0, 1, 3, 2)
    return np.ascontiguousarray(words), np.ascontiguousarray(byte.astype(np.uint8).reshape(r // 512, 16, m))


N, M, V, J, I, K = 512, 512, 1024, 512, 512, 512


def setup_inputs():
    n = np.random.standard_normal
    idx = np.random.permutation(V)[:J]
    idx2 = np.random.permutation(V)[:I]
    fn = mx_kscale(N)
    fm = mx_kscale(M)
    gap = pack_weight(n((N, J)) / fn[:, None], "e4m3")
    wbp = pack_weight(n((M, K)) * 1 / np.sqrt(M) * fm[:, None], "e2m1")
    return {
        "ga_words": gap[0],
        "ga_scales": gap[1],
        "wa": (n((N, K)) * 1 / np.sqrt(N) * fn[:, None]).astype(np.float32),
        "gb": (n((M, I)) / fm[:, None]).astype(np.float32),
        "wb_words": wbp[0],
        "wb_scales": wbp[1],
        "old": (0.5 * n((K, V))).astype(np.float32),
        "offs": striped(idx),
        "offs2": striped(idx2),
    }


def reference(ga_words, ga_scales, wa, gb, wb_words, wb_scales, old, offs, offs2):
    idx = unstriped(offs)
    idx2 = unstriped(offs2)
    gau = unpack_weight(ga_words, ga_scales, "e4m3")
    wbu = unpack_weight(wb_words, wb_scales, "e2m1")
    waq = mxq(f64(wa), 0, "e4m3")
    p = waq.T @ gau
    gbq = mxq(f64(gb), 0, "e5m2")
    q = wbu.T @ gbq
    pg = np.zeros((K, V))
    pg[:, idx] = p
    qg = np.zeros((K, V))
    qg[:, idx2] = q
    y = pg + qg + 0.9 * f64(old)
    words, scales = planes(y)
    return y, words, scales

@@ -1,0 +1,290 @@
+from contextlib import ExitStack
+
+import concourse.mybir as mybir
+from concourse.masks import make_identity
+
+N, M, V, J, K = 512, 512, 1024, 512, 512
+FLOPS = 2 * K * N * J + 2 * K * M * J
+DECAY = 0.9
+
+F32 = mybir.dt.float32
+BF16 = mybir.dt.bfloat16
+I32 = mybir.dt.int32
+U32 = mybir.dt.uint32
+U16 = mybir.dt.uint16
+U8 = mybir.dt.uint8
+E4M3X4 = mybir.dt.float8_e4m3fn_x4
+E5M2X4 = mybir.dt.float8_e5m2_x4
+E2M1X4 = mybir.dt.float4_e2m1fn_x4
+COPY = mybir.ActivationFunctionType.Copy
+ADD = mybir.AluOpType.add
+
+P = 128
+PACK = 4
+SLICES = K // P
+QUADS = 4
+HALVES = 2
+BANK = 512
+VQ = V // QUADS
+
+
+def interleave(copy, grouped, raw):
+    copy(
+        grouped.rearrange("p (c i) t -> p c t i", i=4),
+        raw.rearrange("p t (c i) -> p c t i", i=4),
+    )
+
+
+def tile_list_shared_table_grad_pl_kernel(
+    tc, ga_words, ga_scales, wa, gb, wb_words, wb_scales, old, offs, offs2, out_0, out_1, out_2
+):
+    nc = tc.nc
+    with ExitStack() as ctx:
+        keep = ctx.enter_context(tc.tile_pool(name="keep", bufs=1))
+        ring = ctx.enter_context(tc.tile_pool(name="ring", bufs=2))
+        psum = ctx.enter_context(tc.psum_pool(name="psum", bufs=1))
+
+        def bank(b, name):
+            return psum.tile([P, BANK], F32, name=name, tag=f"bank{b}")
+
+        ga_plane = keep.tile([P, J], U8, name="ga_plane", align_bytes=64)
+        wb_plane = keep.tile([P, K], U8, name="wb_plane", align_bytes=64)
+        nc.vector.memset(ga_plane[:].bitcast(U32), 0)
+        nc.vector.memset(wb_plane[:].bitcast(U32), 0)
+        p_pages = [keep.tile([P, V], F32, name=f"p_page{i}") for i in range(2)]
+        for page in p_pages:
+            nc.vector.memset(page[:].bitcast(I32), 0)
+        ident = keep.tile([P, P], F32, name="ident")
+        make_identity(nc, ident[:])
+
+        def load_rows(src, cols, tag):
+            raw = keep.tile([P, PACK, cols.stop - cols.start], F32, name=tag, tag=tag)
+            nc.sync.dma_start(out=raw[:], in_=src[:, cols].rearrange("(p t) c -> p t c", t=PACK))
+            return raw
+
+        def load_plane(plane, scales):
+            for q in range(QUADS):
+                nc.sync.dma_start(
+                    out=plane[32 * q : 32 * q + 4, :].bitcast(I32),
+                    in_=scales[0, 4 * q : 4 * q + 4, :].bitcast(I32),
+                )
+
+        wa_cols = [slice(0, P), slice(P, 2 * P), slice(2 * P, K)]
+        gb_cols = [slice(0, J // 2), slice(J // 2, J)]
+        wa_raw0 = load_rows(wa, wa_cols[0], "wa_raw0")
+        load_plane(ga_plane, ga_scales)
+        ga_codes = keep.tile([P, J], U32, name="ga_codes", align_bytes=64)
+        nc.sync.dma_start(
+            out=ga_codes[:].bitcast(I32), in_=ga_words[0].rearrange("p n t -> p (n t)").bitcast(I32)
+        )
+        list_p = keep.tile([P, J // 16], U16, name="list_p")
+        nc.sync.dma_start(list_p[:], offs)
+        wa_raw1 = load_rows(wa, wa_cols[1], "wa_raw1")
+        gb_raw0 = load_rows(gb, gb_cols[0], "gb_raw0")
+        gb_raw1 = load_rows(gb, gb_cols[1], "gb_raw1")
+        wb_codes = keep.tile([P, 2 * K], U8, name="wb_codes", align_bytes=64)
+        nc.sync.dma_start(out=wb_codes[:].bitcast(I32), in_=wb_words[0].bitcast(I32))
+        load_plane(wb_plane, wb_scales)
+        wa_raw2 = load_rows(wa, wa_cols[2], "wa_raw2")
+        list_q = keep.tile([P, J // 16], U16, name="list_q")
+        nc.sync.dma_start(list_q[:], offs2)
+        olds = []
+        for s in range(SLICES):
+            old_rows = keep.tile([P, V], F32, name=f"old{s}", tag=f"old{s}")
+            nc.sync.dma_start(out=old_rows[:], in_=old[s * P : (s + 1) * P, :])
+            olds.append(old_rows)
+
+        wa_codes = keep.tile([P, K], U32, name="wa_codes", align_bytes=64)
+        wa_plane = keep.tile([P, K], U8, name="wa_plane", align_bytes=64)
+        gb_codes = keep.tile([P, J], U32, name="gb_codes", align_bytes=64)
+        gb_plane = keep.tile([P, J], U8, name="gb_plane", align_bytes=64)
+        gb_grouped = keep.tile([P, J, PACK], BF16, name="gb_grouped", align_bytes=64)
+
+        def quantise_wa(copy, raw, cols, tag):
+            grouped = keep.tile(
+                [P, cols.stop - cols.start, PACK], BF16, name=tag, tag=tag, align_bytes=64
+            )
+            interleave(copy, grouped[:], raw[:])
+            nc.vector.quantize_mx(
+                out=wa_codes[:, cols].bitcast(E4M3X4),
+                scales=wa_plane[:, cols],
+                in_=grouped[:].rearrange("p c t -> p (c t)"),
+            )
+
+        def stage(acc, width, tag):
+            staged = keep.tile([P, width], F32, name=f"staged_{tag}", tag=tag)
+            nc.scalar.copy(staged[:], acc[:, :width])
+            return staged
+
+        def product_p(s, tokens, b, tag):
+            cols = slice(s * P, (s + 1) * P)
+            width = tokens.stop - tokens.start
+            acc = bank(b, f"p{s}")
+            nc.tensor.matmul_mx(
+                out=acc[:, :width],
+                lhsT=wa_codes[:, cols].bitcast(E4M3X4),
+                lhsT_scale=wa_plane[:, cols],
+                rhs=ga_codes[:, tokens].bitcast(E4M3X4),
+                rhs_scale=ga_plane[:, tokens],
+                start=True,
+                stop=True,
+            )
+            return stage(acc, width, tag)
+
+        def product_q(s, b, tag):
+            acc = bank(b, f"q{s}")
+            nc.tensor.matmul_mx(
+                out=acc[:],
+                lhsT=wb_codes[:, 2 * s * P : 2 * (s + 1) * P].bitcast(E2M1X4),
+                lhsT_scale=wb_plane[:, s * P : (s + 1) * P],
+                rhs=gb_codes[:].bitcast(E5M2X4),
+                rhs_scale=gb_plane[:],
+                start=True,
+                stop=True,
+            )
+            return stage(acc, J, tag)
+
+        def scatter(page, offsets, staged):
+            nc.vector.tensor_copy(page[:].indirect(offsets), staged[:])
+
+        every = slice(0, J)
+        quantise_wa(nc.vector.tensor_copy, wa_raw0, wa_cols[0], "wa_grouped0")
+        scatter(p_pages[0], list_p[:, : J // 32], product_p(0, slice(0, J // 2), 0, "staged_p0"))
+        quantise_wa(nc.scalar.copy, wa_raw1, wa_cols[1], "wa_grouped1")
+        scatter(p_pages[0], list_p[:, J // 32 :], product_p(0, slice(J // 2, J), 1, "wa_raw1"))
+        q_pages = [
+            keep.tile([P, V], F32, name="q_page0", tag="wa_grouped0", align_bytes=64),
+            keep.tile([P, V], F32, name="q_page1", tag="staged_p0"),
+        ]
+        for page in q_pages:
+            nc.gpsimd.memset(page[:], 0.0)
+        interleave(nc.scalar.copy, gb_grouped[:, gb_cols[0], :], gb_raw0[:])
+        interleave(nc.scalar.copy, gb_grouped[:, gb_cols[1], :], gb_raw1[:])
+        nc.vector.quantize_mx(
+            out=gb_codes[:].bitcast(E5M2X4),
+            scales=gb_plane[:],
+            in_=gb_grouped[:].rearrange("p c t -> p (c t)"),
+        )
+        scatter(p_pages[1], list_p[:], product_p(1, every, 2, "gb_raw1"))
+        quantise_wa(nc.scalar.copy, wa_raw2, wa_cols[2], "wa_grouped2")
+        staged_q = {0: product_q(0, 3, "wa_raw2"), 1: product_q(1, 4, "staged_q1")}
+        decayed = [keep.tile([P, V], F32, name=f"decayed{s}") for s in range(SLICES)]
+        staged_p = {}
+        for s in range(SLICES):
+            nc.scalar.activation(decayed[s][:], olds[s][:], COPY, scale=DECAY)
+        for s in range(2, SLICES):
+            staged_p[s] = product_p(s, every, 2 * s + 1, f"old{2 * s - 4}")
+            staged_q[s] = product_q(s, (2 * s + 2) % 8, f"old{2 * s - 3}")
+
+        y_plane = keep.tile([P, VQ], U8, name="y_plane", align_bytes=64)
+        words_out = out_1[0].rearrange("p n t -> p (n t)").bitcast(I32)
+        last = SLICES - 1
+
+        def half_of(rows, h):
+            return rows.rearrange("k (q h v) -> k q h v", q=QUADS, h=HALVES)[:, :, h, :]
+
+        def add_p(s):
+            tag = "wa_grouped2" if s == 0 else f"partial{s}"
+            partial = keep.tile([P, V], F32, name=f"partial{s}", tag=tag, align_bytes=64)
+            nc.gpsimd.tensor_tensor(partial[:], decayed[s][:], p_pages[s % 2][:], ADD)
+            return partial
+
+        def turn(s, y, h):
+            y_t = bank(2 * (s % 2) + h, f"y_t{s}_{h}")
+            for q in range(QUADS):
+                nc.tensor.transpose(y_t[:, q * P : (q + 1) * P], half_of(y[:], h)[:, q, :], ident[:])
+            return y_t
+
+        def add_turned(y_t, src, first):
+            for h in range(HALVES):
+                for q in range(QUADS):
+                    nc.tensor.matmul(
+                        y_t[h][:, q * P : (q + 1) * P],
+                        half_of(src[:], h)[:, q, :],
+                        ident[:],
+                        start=first and q == 0,
+                        stop=not first and q == QUADS - 1,
+                        is_transpose=True,
+                    )
+
+        def round_pairs(copy, y_t, h):
+            pairs = ring.tile([P, 2, P, 2], BF16, name=f"pairs{h}")
+            copy(pairs[:], y_t[:].rearrange("v (g u e) -> v u g e", u=2, e=2))
+            return pairs
+
+        def turn_pairs(s, pairs, grouped, h):
+            turned = bank(4 + 2 * (s % 2) + h, f"turned{s}_{h}")
+            words = pairs[:].rearrange("v u g e -> v (u g e)").bitcast(F32)
+            for u in range(2):
+                nc.tensor.transpose(turned[:, u * P : (u + 1) * P], words[:, u * P : (u + 1) * P], ident[:])
+            nc.scalar.copy(grouped[:, h, :, :], turned[:, : 2 * P].rearrange("g (u v) -> g v u", u=2))
+
+        def finish_slice(s, partial):
+            y = keep.tile([P, V], F32, name=f"y{s}")
+            nc.gpsimd.tensor_tensor(y[:], partial[:], q_pages[s % 2][:], ADD)
+            nc.sync.dma_start(out=out_0[s * P : (s + 1) * P, :], in_=y[:])
+            y_t = [turn(s, y, h) for h in range(HALVES)]
+            pairs = [round_pairs(nc.scalar.copy, y_t[h], h) for h in range(HALVES)]
+            grouped = keep.tile([P, HALVES, P, 2], F32, name=f"grouped{s}", align_bytes=64)
+            for h in range(HALVES):
+                turn_pairs(s, pairs[h], grouped, h)
+            return grouped
+
+        partials = {s: add_p(s) for s in range(2)}
+        groupeds = []
+        for s in range(last):
+            if s == 2:
+                scatter(p_pages[0], list_p[:], staged_p[s])
+                partials[s] = add_p(s)
+            scatter(q_pages[s % 2], list_q[:], staged_q[s])
+            groupeds.append(finish_slice(s, partials[s]))
+        scatter(p_pages[1], list_p[:], staged_p[last])
+        partial = add_p(last)
+        y_t = [bank(2 + h, f"y_t{last}_{h}") for h in range(HALVES)]
+        add_turned(y_t, partial, True)
+        scatter(q_pages[1], list_q[:], staged_q[last])
+        add_turned(y_t, q_pages[1], False)
+
+        y = keep.tile([P, V], F32, name="y_last")
+        for h in range(HALVES):
+            nc.vector.tensor_tensor(
+                half_of(y[:], h), half_of(partial[:], h), half_of(q_pages[1][:], h), ADD
+            )
+            nc.sync.dma_start(out=half_of(out_0[last * P :, :], h), in_=half_of(y[:], h))
+        early_codes = keep.tile(
+            [P, last, VQ], U32, name="early_codes", tag=f"partial{last}", align_bytes=64
+        )
+        for s in range(last):
+            nc.vector.quantize_mx(
+                out=early_codes[:, s, :].bitcast(E4M3X4),
+                scales=y_plane[4 * s :, :],
+                in_=groupeds[s][:].rearrange("g h v u -> g (h v u)").bitcast(BF16),
+            )
+        for q in range(QUADS):
+            nc.sync.dma_start(
+                out=words_out[: 32 * last, q * VQ : (q + 1) * VQ].rearrange("(s p) c -> p s c", s=last),
+                in_=early_codes[32 * q : 32 * (q + 1), :, :].bitcast(I32),
+            )
+        pairs = [
+            round_pairs(copy, y_t[h], h) for h, copy in enumerate((nc.scalar.copy, nc.vector.tensor_copy))
+        ]
+        grouped = keep.tile([P, HALVES, P, 2], F32, name="grouped_last", align_bytes=64)
+        codes = keep.tile([P, VQ], U32, name="last_codes", align_bytes=64)
+        for h in range(HALVES):
+            turn_pairs(last, pairs[h], grouped, h)
+            nc.vector.quantize_mx(
+                out=codes[:, h * P : (h + 1) * P].bitcast(E4M3X4),
+                scales=y_plane[4 * last :, h * P : (h + 1) * P],
+                in_=grouped[:, h, :, :].rearrange("g v u -> g (v u)").bitcast(BF16),
+            )
+        for q in range(QUADS):
+            nc.sync.dma_start(
+                out=words_out[32 * last :, q * VQ : (q + 1) * VQ],
+                in_=codes[32 * q : 32 * (q + 1), :].bitcast(I32),
+            )
+
+        for q in range(QUADS):
+            nc.scalar.dma_start(
+                out=out_2[0, :, q * VQ : (q + 1) * VQ].bitcast(I32),
+                in_=y_plane[32 * q : 32 * q + 16, :].bitcast(I32),
+            )

@@ -49,16 +49,18 @@ def tile_list_shared_table_grad_pl_kernel(
 
         ga_plane = keep.tile([P, J], U8, name="ga_plane", align_bytes=64)
         wb_plane = keep.tile([P, K], U8, name="wb_plane", align_bytes=64)
-        nc.vector.memset(ga_plane[:].bitcast(U32), 0)
-        nc.vector.memset(wb_plane[:].bitcast(U32), 0)
+        nc.gpsimd.memset(ga_plane[:].bitcast(U32), 0)
+        nc.gpsimd.memset(wb_plane[:].bitcast(U32), 0)
         p_pages = [keep.tile([P, V], F32, name=f"p_page{i}") for i in range(2)]
         for page in p_pages:
             nc.vector.memset(page[:].bitcast(I32), 0)
         ident = keep.tile([P, P], F32, name="ident")
         make_identity(nc, ident[:])
+        q_page2 = keep.tile([P, V], F32, name="q_page2")
+        nc.gpsimd.memset(q_page2[:], 0.0)
 
         def load_rows(src, cols, tag):
-            raw = keep.tile([P, PACK, cols.stop - cols.start], F32, name=tag, tag=tag)
+            raw = keep.tile([P, PACK, cols.stop - cols.start], F32, name=tag, tag=tag, align_bytes=64)
             nc.sync.dma_start(out=raw[:], in_=src[:, cols].rearrange("(p t) c -> p t c", t=PACK))
             return raw
 
@@ -80,19 +82,23 @@ def tile_list_shared_table_grad_pl_kernel(
         list_p = keep.tile([P, J // 16], U16, name="list_p")
         nc.sync.dma_start(list_p[:], offs)
         wa_raw1 = load_rows(wa, wa_cols[1], "wa_raw1")
+        wa_raw2 = load_rows(wa, wa_cols[2], "wa_raw2")
+        olds = [keep.tile([P, V], F32, name=f"old{s}", tag=f"old{s}", align_bytes=64) for s in range(SLICES)]
+
+        def load_old(s):
+            nc.sync.dma_start(out=olds[s][:], in_=old[s * P : (s + 1) * P, :])
+
+        load_old(0)
         gb_raw0 = load_rows(gb, gb_cols[0], "gb_raw0")
         gb_raw1 = load_rows(gb, gb_cols[1], "gb_raw1")
+        load_old(1)
+        load_old(2)
         wb_codes = keep.tile([P, 2 * K], U8, name="wb_codes", align_bytes=64)
         nc.sync.dma_start(out=wb_codes[:].bitcast(I32), in_=wb_words[0].bitcast(I32))
         load_plane(wb_plane, wb_scales)
-        wa_raw2 = load_rows(wa, wa_cols[2], "wa_raw2")
         list_q = keep.tile([P, J // 16], U16, name="list_q")
         nc.sync.dma_start(list_q[:], offs2)
-        olds = []
-        for s in range(SLICES):
-            old_rows = keep.tile([P, V], F32, name=f"old{s}", tag=f"old{s}")
-            nc.sync.dma_start(out=old_rows[:], in_=old[s * P : (s + 1) * P, :])
-            olds.append(old_rows)
+        load_old(3)
 
         wa_codes = keep.tile([P, K], U32, name="wa_codes", align_bytes=64)
         wa_plane = keep.tile([P, K], U8, name="wa_plane", align_bytes=64)
@@ -111,25 +117,25 @@ def tile_list_shared_table_grad_pl_kernel(
                 in_=grouped[:].rearrange("p c t -> p (c t)"),
             )
 
-        def stage(acc, width, tag):
-            staged = keep.tile([P, width], F32, name=f"staged_{tag}", tag=tag)
-            nc.scalar.copy(staged[:], acc[:, :width])
+        def stage(acc, width, tag, copy=nc.scalar.copy):
+            staged = keep.tile([P, width], F32, name=f"staged_{tag}", tag=tag, align_bytes=64)
+            copy(staged[:], acc[:, :width])
             return staged
 
-        def product_p(s, tokens, b, tag):
+        def product_p(s, edges, b, tag, copy=nc.scalar.copy):
             cols = slice(s * P, (s + 1) * P)
-            width = tokens.stop - tokens.start
             acc = bank(b, f"p{s}")
-            nc.tensor.matmul_mx(
-                out=acc[:, :width],
-                lhsT=wa_codes[:, cols].bitcast(E4M3X4),
-                lhsT_scale=wa_plane[:, cols],
-                rhs=ga_codes[:, tokens].bitcast(E4M3X4),
-                rhs_scale=ga_plane[:, tokens],
-                start=True,
-                stop=True,
-            )
-            return stage(acc, width, tag)
+            for lo, hi in zip(edges, edges[1:]):
+                nc.tensor.matmul_mx(
+                    out=acc[:, lo - edges[0] : hi - edges[0]],
+                    lhsT=wa_codes[:, cols].bitcast(E4M3X4),
+                    lhsT_scale=wa_plane[:, cols],
+                    rhs=ga_codes[:, lo:hi].bitcast(E4M3X4),
+                    rhs_scale=ga_plane[:, lo:hi],
+                    start=True,
+                    stop=True,
+                )
+            return stage(acc, edges[-1] - edges[0], tag, copy)
 
         def product_q(s, b, tag):
             acc = bank(b, f"q{s}")
@@ -147,35 +153,18 @@ def tile_list_shared_table_grad_pl_kernel(
         def scatter(page, offsets, staged):
             nc.vector.tensor_copy(page[:].indirect(offsets), staged[:])
 
-        every = slice(0, J)
+        every = (0, J)
         quantise_wa(nc.vector.tensor_copy, wa_raw0, wa_cols[0], "wa_grouped0")
-        scatter(p_pages[0], list_p[:, : J // 32], product_p(0, slice(0, J // 2), 0, "staged_p0"))
+        scatter(p_pages[0], list_p[:, : P // 16], product_p(0, (0, P), 0, "staged_p0", nc.vector.tensor_copy))
         quantise_wa(nc.scalar.copy, wa_raw1, wa_cols[1], "wa_grouped1")
-        scatter(p_pages[0], list_p[:, J // 32 :], product_p(0, slice(J // 2, J), 1, "wa_raw1"))
+        scatter(p_pages[0], list_p[:, P // 16 :], product_p(0, (P, 2 * P, J), 1, "wa_raw1"))
         q_pages = [
             keep.tile([P, V], F32, name="q_page0", tag="wa_grouped0", align_bytes=64),
-            keep.tile([P, V], F32, name="q_page1", tag="staged_p0"),
+            keep.tile([P, V], F32, name="q_page1", tag="staged_p0", align_bytes=64),
+            q_page2,
         ]
-        for page in q_pages:
+        for page in q_pages[:2]:
             nc.gpsimd.memset(page[:], 0.0)
-        interleave(nc.scalar.copy, gb_grouped[:, gb_cols[0], :], gb_raw0[:])
-        interleave(nc.scalar.copy, gb_grouped[:, gb_cols[1], :], gb_raw1[:])
-        nc.vector.quantize_mx(
-            out=gb_codes[:].bitcast(E5M2X4),
-            scales=gb_plane[:],
-            in_=gb_grouped[:].rearrange("p c t -> p (c t)"),
-        )
-        scatter(p_pages[1], list_p[:], product_p(1, every, 2, "gb_raw1"))
-        quantise_wa(nc.scalar.copy, wa_raw2, wa_cols[2], "wa_grouped2")
-        staged_q = {0: product_q(0, 3, "wa_raw2"), 1: product_q(1, 4, "staged_q1")}
-        decayed = [keep.tile([P, V], F32, name=f"decayed{s}") for s in range(SLICES)]
-        staged_p = {}
-        for s in range(SLICES):
-            nc.scalar.activation(decayed[s][:], olds[s][:], COPY, scale=DECAY)
-        for s in range(2, SLICES):
-            staged_p[s] = product_p(s, every, 2 * s + 1, f"old{2 * s - 4}")
-            staged_q[s] = product_q(s, (2 * s + 2) % 8, f"old{2 * s - 3}")
-
         y_plane = keep.tile([P, VQ], U8, name="y_plane", align_bytes=64)
         words_out = out_1[0].rearrange("p n t -> p (n t)").bitcast(I32)
         last = SLICES - 1
@@ -183,10 +172,20 @@ def tile_list_shared_table_grad_pl_kernel(
         def half_of(rows, h):
             return rows.rearrange("k (q h v) -> k q h v", q=QUADS, h=HALVES)[:, :, h, :]
 
-        def add_p(s):
-            tag = "wa_grouped2" if s == 0 else f"partial{s}"
-            partial = keep.tile([P, V], F32, name=f"partial{s}", tag=tag, align_bytes=64)
-            nc.gpsimd.tensor_tensor(partial[:], decayed[s][:], p_pages[s % 2][:], ADD)
+        def decay(s):
+            decayed = keep.tile([P, V], F32, name=f"decayed{s}", tag=f"decayed{s}", align_bytes=64)
+            nc.scalar.activation(decayed[:], olds[s][:], COPY, scale=DECAY)
+            return decayed
+
+        def add_p(s, decayed):
+            partial = keep.tile([P, V], F32, name=f"partial{s}", tag=f"partial{s}", align_bytes=64)
+            if s == last:
+                for h in range(HALVES):
+                    nc.gpsimd.tensor_tensor(
+                        half_of(partial[:], h), half_of(decayed[:], h), half_of(p_pages[1][:], h), ADD
+                    )
+            else:
+                nc.gpsimd.tensor_tensor(partial[:], decayed[:], p_pages[s % 2][:], ADD)
             return partial
 
         def turn(s, y, h):
@@ -221,7 +220,7 @@ def tile_list_shared_table_grad_pl_kernel(
 
         def finish_slice(s, partial):
             y = keep.tile([P, V], F32, name=f"y{s}")
-            nc.gpsimd.tensor_tensor(y[:], partial[:], q_pages[s % 2][:], ADD)
+            nc.gpsimd.tensor_tensor(y[:], partial[:], q_pages[s][:], ADD)
             nc.sync.dma_start(out=out_0[s * P : (s + 1) * P, :], in_=y[:])
             y_t = [turn(s, y, h) for h in range(HALVES)]
             pairs = [round_pairs(nc.scalar.copy, y_t[h], h) for h in range(HALVES)]
@@ -230,25 +229,38 @@ def tile_list_shared_table_grad_pl_kernel(
                 turn_pairs(s, pairs[h], grouped, h)
             return grouped
 
-        partials = {s: add_p(s) for s in range(2)}
+        quantise_wa(nc.scalar.copy, wa_raw2, wa_cols[2], "wa_grouped1")
+        scatter(p_pages[1], list_p[:], product_p(1, every, 2, "wa_raw2"))
+        partials = [add_p(0, decay(0))]
+        interleave(nc.scalar.copy, gb_grouped[:, gb_cols[0], :], gb_raw0[:])
+        interleave(nc.scalar.copy, gb_grouped[:, gb_cols[1], :], gb_raw1[:])
+        nc.vector.quantize_mx(
+            out=gb_codes[:].bitcast(E5M2X4),
+            scales=gb_plane[:],
+            in_=gb_grouped[:].rearrange("p c t -> p (c t)"),
+        )
+        scatter(p_pages[0], list_p[:], product_p(2, every, 3, "gb_raw1"))
+        partials.append(add_p(1, decay(1)))
+        partials.append(add_p(2, decay(2)))
+        staged_q = [product_q(s, 4, f"staged_q{s}" if s else "decayed0") for s in range(last)]
+        decayed_last = decay(last)
+        staged_p3 = product_p(last, every, 4, "staged_p3")
+        staged_q.append(product_q(last, 4, "old3"))
         groupeds = []
         for s in range(last):
-            if s == 2:
-                scatter(p_pages[0], list_p[:], staged_p[s])
-                partials[s] = add_p(s)
-            scatter(q_pages[s % 2], list_q[:], staged_q[s])
+            scatter(q_pages[s], list_q[:], staged_q[s])
             groupeds.append(finish_slice(s, partials[s]))
-        scatter(p_pages[1], list_p[:], staged_p[last])
-        partial = add_p(last)
-        y_t = [bank(2 + h, f"y_t{last}_{h}") for h in range(HALVES)]
+        scatter(p_pages[1], list_p[:], staged_p3)
+        partial = add_p(last, decayed_last)
+        y_t = [bank(b, f"y_t{last}_{b}") for b in (1, 4)]
         add_turned(y_t, partial, True)
-        scatter(q_pages[1], list_q[:], staged_q[last])
-        add_turned(y_t, q_pages[1], False)
+        scatter(q_pages[0], list_q[:], staged_q[last])
+        add_turned(y_t, q_pages[0], False)
 
         y = keep.tile([P, V], F32, name="y_last")
         for h in range(HALVES):
             nc.vector.tensor_tensor(
-                half_of(y[:], h), half_of(partial[:], h), half_of(q_pages[1][:], h), ADD
+                half_of(y[:], h), half_of(partial[:], h), half_of(q_pages[0][:], h), ADD
             )
             nc.sync.dma_start(out=half_of(out_0[last * P :, :], h), in_=half_of(y[:], h))
         early_codes = keep.tile(
@@ -265,9 +277,7 @@ def tile_list_shared_table_grad_pl_kernel(
                 out=words_out[: 32 * last, q * VQ : (q + 1) * VQ].rearrange("(s p) c -> p s c", s=last),
                 in_=early_codes[32 * q : 32 * (q + 1), :, :].bitcast(I32),
             )
-        pairs = [
-            round_pairs(copy, y_t[h], h) for h, copy in enumerate((nc.scalar.copy, nc.vector.tensor_copy))
-        ]
+        pairs = [round_pairs(nc.scalar.copy, y_t[h], h) for h in range(HALVES)]
         grouped = keep.tile([P, HALVES, P, 2], F32, name="grouped_last", align_bytes=64)
         codes = keep.tile([P, VQ], U32, name="last_codes", align_bytes=64)
         for h in range(HALVES):

@@ -179,13 +179,7 @@ def tile_list_shared_table_grad_pl_kernel(
 
         def add_p(s, decayed):
             partial = keep.tile([P, V], F32, name=f"partial{s}", tag=f"partial{s}", align_bytes=64)
-            if s == last:
-                for h in range(HALVES):
-                    nc.gpsimd.tensor_tensor(
-                        half_of(partial[:], h), half_of(decayed[:], h), half_of(p_pages[1][:], h), ADD
-                    )
-            else:
-                nc.gpsimd.tensor_tensor(partial[:], decayed[:], p_pages[s % 2][:], ADD)
+            nc.gpsimd.tensor_tensor(partial[:], decayed[:], p_pages[s % 2][:], ADD)
             return partial
 
         def turn(s, y, h):
@@ -194,7 +188,7 @@ def tile_list_shared_table_grad_pl_kernel(
                 nc.tensor.transpose(y_t[:, q * P : (q + 1) * P], half_of(y[:], h)[:, q, :], ident[:])
             return y_t
 
-        def add_turned(y_t, src, first):
+        def add_turned(y_t, src, first, final):
             for h in range(HALVES):
                 for q in range(QUADS):
                     nc.tensor.matmul(
@@ -202,7 +196,7 @@ def tile_list_shared_table_grad_pl_kernel(
                         half_of(src[:], h)[:, q, :],
                         ident[:],
                         start=first and q == 0,
-                        stop=not first and q == QUADS - 1,
+                        stop=final and q == QUADS - 1,
                         is_transpose=True,
                     )
 
@@ -220,7 +214,10 @@ def tile_list_shared_table_grad_pl_kernel(
 
         def finish_slice(s, partial):
             y = keep.tile([P, V], F32, name=f"y{s}")
-            nc.gpsimd.tensor_tensor(y[:], partial[:], q_pages[s][:], ADD)
+            for h in range(HALVES):
+                nc.gpsimd.tensor_tensor(
+                    half_of(y[:], h), half_of(partial[:], h), half_of(q_pages[s][:], h), ADD
+                )
             nc.sync.dma_start(out=out_0[s * P : (s + 1) * P, :], in_=y[:])
             y_t = [turn(s, y, h) for h in range(HALVES)]
             pairs = [round_pairs(nc.scalar.copy, y_t[h], h) for h in range(HALVES)]
@@ -242,20 +239,21 @@ def tile_list_shared_table_grad_pl_kernel(
         scatter(p_pages[0], list_p[:], product_p(2, every, 3, "gb_raw1"))
         partials.append(add_p(1, decay(1)))
         partials.append(add_p(2, decay(2)))
-        staged_q = [product_q(s, 4, f"staged_q{s}" if s else "decayed0") for s in range(last)]
+        staged_q = [product_q(s, 4 + s, f"staged_q{s}" if s else "decayed0") for s in range(last)]
         decayed_last = decay(last)
-        staged_p3 = product_p(last, every, 4, "staged_p3")
-        staged_q.append(product_q(last, 4, "old3"))
+        staged_p3 = product_p(last, every, 6, "staged_p3")
+        staged_q.append(product_q(last, 7, "old3"))
         groupeds = []
         for s in range(last):
             scatter(q_pages[s], list_q[:], staged_q[s])
             groupeds.append(finish_slice(s, partials[s]))
         scatter(p_pages[1], list_p[:], staged_p3)
         partial = add_p(last, decayed_last)
-        y_t = [bank(b, f"y_t{last}_{b}") for b in (1, 4)]
-        add_turned(y_t, partial, True)
+        y_t = [bank(1 - h, f"y_t{last}_{h}") for h in range(HALVES)]
+        add_turned(y_t, decayed_last, True, False)
+        add_turned(y_t, p_pages[1], False, False)
         scatter(q_pages[0], list_q[:], staged_q[last])
-        add_turned(y_t, q_pages[0], False)
+        add_turned(y_t, q_pages[0], False, True)
 
         y = keep.tile([P, V], F32, name="y_last")
         for h in range(HALVES):

from contextlib import ExitStack

import concourse.mybir as mybir
from concourse.masks import make_identity

N, M, V, J, K = 512, 512, 1024, 512, 512
FLOPS = 2 * K * N * J + 2 * K * M * J
DECAY = 0.9

F32 = mybir.dt.float32
BF16 = mybir.dt.bfloat16
I32 = mybir.dt.int32
U32 = mybir.dt.uint32
U16 = mybir.dt.uint16
U8 = mybir.dt.uint8
E4M3X4 = mybir.dt.float8_e4m3fn_x4
E5M2X4 = mybir.dt.float8_e5m2_x4
E2M1X4 = mybir.dt.float4_e2m1fn_x4
COPY = mybir.ActivationFunctionType.Copy
ADD = mybir.AluOpType.add

P = 128
PACK = 4
SLICES = K // P
QUADS = 4
HALVES = 2
BANK = 512
VQ = V // QUADS


def interleave(copy, grouped, raw):
    copy(
        grouped.rearrange("p (c i) t -> p c t i", i=4),
        raw.rearrange("p t (c i) -> p c t i", i=4),
    )


def tile_list_shared_table_grad_pl_kernel(
    tc, ga_words, ga_scales, wa, gb, wb_words, wb_scales, old, offs, offs2, out_0, out_1, out_2
):
    nc = tc.nc
    with ExitStack() as ctx:
        keep = ctx.enter_context(tc.tile_pool(name="keep", bufs=1))
        ring = ctx.enter_context(tc.tile_pool(name="ring", bufs=2))
        psum = ctx.enter_context(tc.psum_pool(name="psum", bufs=1))

        def bank(b, name):
            return psum.tile([P, BANK], F32, name=name, tag=f"bank{b}")

        ga_plane = keep.tile([P, J], U8, name="ga_plane", align_bytes=64)
        wb_plane = keep.tile([P, K], U8, name="wb_plane", align_bytes=64)
        nc.gpsimd.memset(ga_plane[:].bitcast(U32), 0)
        nc.gpsimd.memset(wb_plane[:].bitcast(U32), 0)
        p_pages = [keep.tile([P, V], F32, name=f"p_page{i}") for i in range(2)]
        for page in p_pages:
            nc.vector.memset(page[:].bitcast(I32), 0)
        ident = keep.tile([P, P], F32, name="ident")
        make_identity(nc, ident[:])
        q_page2 = keep.tile([P, V], F32, name="q_page2")
        nc.gpsimd.memset(q_page2[:], 0.0)

        def load_rows(src, cols, tag):
            raw = keep.tile([P, PACK, cols.stop - cols.start], F32, name=tag, tag=tag, align_bytes=64)
            nc.sync.dma_start(out=raw[:], in_=src[:, cols].rearrange("(p t) c -> p t c", t=PACK))
            return raw

        def load_plane(plane, scales):
            for q in range(QUADS):
                nc.sync.dma_start(
                    out=plane[32 * q : 32 * q + 4, :].bitcast(I32),
                    in_=scales[0, 4 * q : 4 * q + 4, :].bitcast(I32),
                )

        wa_cols = [slice(0, P), slice(P, 2 * P), slice(2 * P, K)]
        gb_cols = [slice(0, J // 2), slice(J // 2, J)]
        wa_raw0 = load_rows(wa, wa_cols[0], "wa_raw0")
        load_plane(ga_plane, ga_scales)
        ga_codes = keep.tile([P, J], U32, name="ga_codes", align_bytes=64)
        nc.sync.dma_start(
            out=ga_codes[:].bitcast(I32), in_=ga_words[0].rearrange("p n t -> p (n t)").bitcast(I32)
        )
        list_p = keep.tile([P, J // 16], U16, name="list_p")
        nc.sync.dma_start(list_p[:], offs)
        wa_raw1 = load_rows(wa, wa_cols[1], "wa_raw1")
        wa_raw2 = load_rows(wa, wa_cols[2], "wa_raw2")
        olds = [keep.tile([P, V], F32, name=f"old{s}", tag=f"old{s}", align_bytes=64) for s in range(SLICES)]

        def load_old(s):
            nc.sync.dma_start(out=olds[s][:], in_=old[s * P : (s + 1) * P, :])

        load_old(0)
        gb_raw0 = load_rows(gb, gb_cols[0], "gb_raw0")
        gb_raw1 = load_rows(gb, gb_cols[1], "gb_raw1")
        load_old(1)
        load_old(2)
        wb_codes = keep.tile([P, 2 * K], U8, name="wb_codes", align_bytes=64)
        nc.sync.dma_start(out=wb_codes[:].bitcast(I32), in_=wb_words[0].bitcast(I32))
        load_plane(wb_plane, wb_scales)
        list_q = keep.tile([P, J // 16], U16, name="list_q")
        nc.sync.dma_start(list_q[:], offs2)
        load_old(3)

        wa_codes = keep.tile([P, K], U32, name="wa_codes", align_bytes=64)
        wa_plane = keep.tile([P, K], U8, name="wa_plane", align_bytes=64)
        gb_codes = keep.tile([P, J], U32, name="gb_codes", align_bytes=64)
        gb_plane = keep.tile([P, J], U8, name="gb_plane", align_bytes=64)
        gb_grouped = keep.tile([P, J, PACK], BF16, name="gb_grouped", align_bytes=64)

        def quantise_wa(copy, raw, cols, tag):
            grouped = keep.tile(
                [P, cols.stop - cols.start, PACK], BF16, name=tag, tag=tag, align_bytes=64
            )
            interleave(copy, grouped[:], raw[:])
            nc.vector.quantize_mx(
                out=wa_codes[:, cols].bitcast(E4M3X4),
                scales=wa_plane[:, cols],
                in_=grouped[:].rearrange("p c t -> p (c t)"),
            )

        def stage(acc, width, tag, copy=nc.scalar.copy):
            staged = keep.tile([P, width], F32, name=f"staged_{tag}", tag=tag, align_bytes=64)
            copy(staged[:], acc[:, :width])
            return staged

        def product_p(s, edges, b, tag, copy=nc.scalar.copy):
            cols = slice(s * P, (s + 1) * P)
            acc = bank(b, f"p{s}")
            for lo, hi in zip(edges, edges[1:]):
                nc.tensor.matmul_mx(
                    out=acc[:, lo - edges[0] : hi - edges[0]],
                    lhsT=wa_codes[:, cols].bitcast(E4M3X4),
                    lhsT_scale=wa_plane[:, cols],
                    rhs=ga_codes[:, lo:hi].bitcast(E4M3X4),
                    rhs_scale=ga_plane[:, lo:hi],
                    start=True,
                    stop=True,
                )
            return stage(acc, edges[-1] - edges[0], tag, copy)

        def product_q(s, b, tag):
            acc = bank(b, f"q{s}")
            nc.tensor.matmul_mx(
                out=acc[:],
                lhsT=wb_codes[:, 2 * s * P : 2 * (s + 1) * P].bitcast(E2M1X4),
                lhsT_scale=wb_plane[:, s * P : (s + 1) * P],
                rhs=gb_codes[:].bitcast(E5M2X4),
                rhs_scale=gb_plane[:],
                start=True,
                stop=True,
            )
            return stage(acc, J, tag)

        def scatter(page, offsets, staged):
            nc.vector.tensor_copy(page[:].indirect(offsets), staged[:])

        every = (0, J)
        quantise_wa(nc.vector.tensor_copy, wa_raw0, wa_cols[0], "wa_grouped0")
        scatter(p_pages[0], list_p[:, : P // 16], product_p(0, (0, P), 0, "staged_p0", nc.vector.tensor_copy))
        quantise_wa(nc.scalar.copy, wa_raw1, wa_cols[1], "wa_grouped1")
        scatter(p_pages[0], list_p[:, P // 16 :], product_p(0, (P, 2 * P, J), 1, "wa_raw1"))
        q_pages = [
            keep.tile([P, V], F32, name="q_page0", tag="wa_grouped0", align_bytes=64),
            keep.tile([P, V], F32, name="q_page1", tag="staged_p0", align_bytes=64),
            q_page2,
        ]
        for page in q_pages[:2]:
            nc.gpsimd.memset(page[:], 0.0)
        y_plane = keep.tile([P, VQ], U8, name="y_plane", align_bytes=64)
        words_out = out_1[0].rearrange("p n t -> p (n t)").bitcast(I32)
        last = SLICES - 1

        def half_of(rows, h):
            return rows.rearrange("k (q h v) -> k q h v", q=QUADS, h=HALVES)[:, :, h, :]

        def decay(s):
            decayed = keep.tile([P, V], F32, name=f"decayed{s}", tag=f"decayed{s}", align_bytes=64)
            nc.scalar.activation(decayed[:], olds[s][:], COPY, scale=DECAY)
            return decayed

        def add_p(s, decayed):
            partial = keep.tile([P, V], F32, name=f"partial{s}", tag=f"partial{s}", align_bytes=64)
            nc.gpsimd.tensor_tensor(partial[:], decayed[:], p_pages[s % 2][:], ADD)
            return partial

        def turn(s, y, h):
            y_t = bank(2 * (s % 2) + h, f"y_t{s}_{h}")
            for q in range(QUADS):
                nc.tensor.transpose(y_t[:, q * P : (q + 1) * P], half_of(y[:], h)[:, q, :], ident[:])
            return y_t

        def add_turned(y_t, src, first, final):
            for h in range(HALVES):
                for q in range(QUADS):
                    nc.tensor.matmul(
                        y_t[h][:, q * P : (q + 1) * P],
                        half_of(src[:], h)[:, q, :],
                        ident[:],
                        start=first and q == 0,
                        stop=final and q == QUADS - 1,
                        is_transpose=True,
                    )

        def round_pairs(copy, y_t, h):
            pairs = ring.tile([P, 2, P, 2], BF16, name=f"pairs{h}")
            copy(pairs[:], y_t[:].rearrange("v (g u e) -> v u g e", u=2, e=2))
            return pairs

        def turn_pairs(s, pairs, grouped, h):
            turned = bank(4 + 2 * (s % 2) + h, f"turned{s}_{h}")
            words = pairs[:].rearrange("v u g e -> v (u g e)").bitcast(F32)
            for u in range(2):
                nc.tensor.transpose(turned[:, u * P : (u + 1) * P], words[:, u * P : (u + 1) * P], ident[:])
            nc.scalar.copy(grouped[:, h, :, :], turned[:, : 2 * P].rearrange("g (u v) -> g v u", u=2))

        def finish_slice(s, partial):
            y = keep.tile([P, V], F32, name=f"y{s}")
            for h in range(HALVES):
                nc.gpsimd.tensor_tensor(
                    half_of(y[:], h), half_of(partial[:], h), half_of(q_pages[s][:], h), ADD
                )
            nc.sync.dma_start(out=out_0[s * P : (s + 1) * P, :], in_=y[:])
            y_t = [turn(s, y, h) for h in range(HALVES)]
            pairs = [round_pairs(nc.scalar.copy, y_t[h], h) for h in range(HALVES)]
            grouped = keep.tile([P, HALVES, P, 2], F32, name=f"grouped{s}", align_bytes=64)
            for h in range(HALVES):
                turn_pairs(s, pairs[h], grouped, h)
            return grouped

        quantise_wa(nc.scalar.copy, wa_raw2, wa_cols[2], "wa_grouped1")
        scatter(p_pages[1], list_p[:], product_p(1, every, 2, "wa_raw2"))
        partials = [add_p(0, decay(0))]
        interleave(nc.scalar.copy, gb_grouped[:, gb_cols[0], :], gb_raw0[:])
        interleave(nc.scalar.copy, gb_grouped[:, gb_cols[1], :], gb_raw1[:])
        nc.vector.quantize_mx(
            out=gb_codes[:].bitcast(E5M2X4),
            scales=gb_plane[:],
            in_=gb_grouped[:].rearrange("p c t -> p (c t)"),
        )
        scatter(p_pages[0], list_p[:], product_p(2, every, 3, "gb_raw1"))
        partials.append(add_p(1, decay(1)))
        partials.append(add_p(2, decay(2)))
        staged_q = [product_q(s, 4 + s, f"staged_q{s}" if s else "decayed0") for s in range(last)]
        decayed_last = decay(last)
        staged_p3 = product_p(last, every, 6, "staged_p3")
        staged_q.append(product_q(last, 7, "old3"))
        groupeds = []
        for s in range(last):
            scatter(q_pages[s], list_q[:], staged_q[s])
            groupeds.append(finish_slice(s, partials[s]))
        scatter(p_pages[1], list_p[:], staged_p3)
        partial = add_p(last, decayed_last)
        y_t = [bank(1 - h, f"y_t{last}_{h}") for h in range(HALVES)]
        add_turned(y_t, decayed_last, True, False)
        add_turned(y_t, p_pages[1], False, False)
        scatter(q_pages[0], list_q[:], staged_q[last])
        add_turned(y_t, q_pages[0], False, True)

        y = keep.tile([P, V], F32, name="y_last")
        for h in range(HALVES):
            nc.vector.tensor_tensor(
                half_of(y[:], h), half_of(partial[:], h), half_of(q_pages[0][:], h), ADD
            )
            nc.sync.dma_start(out=half_of(out_0[last * P :, :], h), in_=half_of(y[:], h))
        early_codes = keep.tile(
            [P, last, VQ], U32, name="early_codes", tag=f"partial{last}", align_bytes=64
        )
        for s in range(last):
            nc.vector.quantize_mx(
                out=early_codes[:, s, :].bitcast(E4M3X4),
                scales=y_plane[4 * s :, :],
                in_=groupeds[s][:].rearrange("g h v u -> g (h v u)").bitcast(BF16),
            )
        for q in range(QUADS):
            nc.sync.dma_start(
                out=words_out[: 32 * last, q * VQ : (q + 1) * VQ].rearrange("(s p) c -> p s c", s=last),
                in_=early_codes[32 * q : 32 * (q + 1), :, :].bitcast(I32),
            )
        pairs = [round_pairs(nc.scalar.copy, y_t[h], h) for h in range(HALVES)]
        grouped = keep.tile([P, HALVES, P, 2], F32, name="grouped_last", align_bytes=64)
        codes = keep.tile([P, VQ], U32, name="last_codes", align_bytes=64)
        for h in range(HALVES):
            turn_pairs(last, pairs[h], grouped, h)
            nc.vector.quantize_mx(
                out=codes[:, h * P : (h + 1) * P].bitcast(E4M3X4),
                scales=y_plane[4 * last :, h * P : (h + 1) * P],
                in_=grouped[:, h, :, :].rearrange("g v u -> g (v u)").bitcast(BF16),
            )
        for q in range(QUADS):
            nc.sync.dma_start(
                out=words_out[32 * last :, q * VQ : (q + 1) * VQ],
                in_=codes[32 * q : 32 * (q + 1), :].bitcast(I32),
            )

        for q in range(QUADS):
            nc.scalar.dma_start(
                out=out_2[0, :, q * VQ : (q + 1) * VQ].bitcast(I32),
                in_=y_plane[32 * q : 32 * q + 16, :].bitcast(I32),
            )
